import numpy as np
import ml_dtypes


def mxq(x, axis, fmt="e4m3"):
    dtype, down = {"e4m3": (ml_dtypes.float8_e4m3fn, 7), "e5m2": (ml_dtypes.float8_e5m2, 14)}[fmt]
    v = np.moveaxis(np.asarray(x, np.float32).astype(ml_dtypes.bfloat16).astype(np.float64), axis, -1)
    blocks = v.reshape(v.shape[:-1] + (-1, 32))
    amax = np.abs(blocks).max(-1, keepdims=True)
    byte = np.maximum(np.where(amax > 0, np.frexp(amax)[1] - 1 + 127, 0) - down, 1)
    scale = np.exp2(byte - 127.0)
    codes = (blocks / scale).astype(np.float32).astype(dtype).astype(np.float64)
    return np.moveaxis((codes * scale).reshape(v.shape), -1, axis)


WIDE = False


def mx_kscale(k):
    if not WIDE:
        return np.ones(k)
    levels = np.array([24, -24, 12, -12, 0])
    if k % 512:
        return np.exp2(np.random.permutation(np.resize(levels, k // 32))).repeat(32)
    a = np.empty((k // 512, 16))
    for p in range(k // 512):
        a[p, :8] = np.random.permutation(np.resize(levels, 8))
        for g in range(8):
            far = levels[np.abs(levels - a[p, g]) >= 10]
            a[p, g + 8] = far[np.random.randint(len(far))]
    return np.exp2(a.ravel()).repeat(32)


def f64(x):
    return np.asarray(x).astype(np.float64)


def striped8(idx):
    return np.concatenate([v.reshape(-1, 16).T for v in idx]).astype(np.uint16)


def unstriped8(offs):
    return np.stack([offs[16 * g:16 * g + 16].T.reshape(-1) for g in range(8)]).astype(np.int64)


E2M1 = np.array([0.0, 0.5, 1.0, 1.5, 2.0, 3.0, 4.0, 6.0, -0.0, -0.5, -1.0, -1.5, -2.0, -3.0, -4.0, -6.0])


def pack_weight(w, fmt):
    k, n = w.shape
    w = f64(np.asarray(w, np.float32).astype(ml_dtypes.bfloat16)).reshape(k // 32, 32, n)
    amax = np.abs(w).max(1)
    if fmt == "e4m3":
        byte = np.frexp(amax)[1] - 1 + 127 - 7
    else:
        mant, ex = np.frexp(amax / 6.0)
        byte = np.where(mant > 0.5, ex, ex - 1) + 127
    byte = np.clip(np.where(amax > 0, byte, 1), 1, 254)
    scaled = (w * np.exp2(127.0 - byte)[:, None, :]).reshape(k, n).astype(np.float32)
    by_word = np.ascontiguousarray(scaled.reshape(k // 512, 128, 4, n).transpose(0, 1, 3, 2))
    if fmt == "e4m3":
        words = by_word.astype(ml_dtypes.float8_e4m3fn).view(np.uint8)
    else:
        c = by_word.astype(ml_dtypes.float4_e2m1fn).view(np.uint8) & 0xF
        words = (c[..., 0::2] | (c[..., 1::2] << 4)).reshape(k // 512, 128, 2 * n)
    return np.ascontiguousarray(words), np.ascontiguousarray(byte.astype(np.uint8).reshape(k // 512, 16, n))


def unpack_weight(words, scales, fmt):
    g, _, n = scales.shape
    words = np.ascontiguousarray(words).reshape(g, 128, n, -1)
    if fmt == "e4m3":
        vals = words.view(ml_dtypes.float8_e4m3fn).astype(np.float64)
    else:
        nib = np.empty((g, 128, n, 4), np.uint8)
        nib[..., 0::2] = words & 0xF
        nib[..., 1::2] = words >> 4
        vals = E2M1[nib]
    vals = vals * np.repeat(np.exp2(scales.astype(np.float64) - 127.0), 8, axis=1)[..., None]
    return vals.transpose(0, 1, 3, 2).reshape(g * 512, n)


def planes(y):
    n, m = y.shape
    v = y.astype(np.float32).astype(ml_dtypes.bfloat16).astype(np.float64).reshape(n // 32, 32, m)
    top = np.abs(v).max(1)
    byte = np.clip(np.where(top > 0, np.frexp(top)[1] - 1 + 127 - 7, 1), 1, 254)
    codes = (v * np.exp2(127.0 - byte)[:, None, :]).reshape(n, m).astype(np.float32).astype(ml_dtypes.float8_e4m3fn).view(np.uint8)
    words = codes.reshape(n // 512, 128, 4, m).transpose(0, 1, 3, 2)
    return np.ascontiguousarray(words), np.ascontiguousarray(byte.astype(np.uint8).reshape(n // 512, 16, m))


K, L, N, T, J = 512, 512, 512, 2048, 1024


def setup_inputs():
    n = np.random.standard_normal
    s = mx_kscale(K)[:, None]
    s2 = mx_kscale(L)[:, None]
    p_wa = pack_weight(n((K, N)) / np.sqrt(K) / s, "e4m3")
    p_wb = pack_weight(n((L, N)) / np.sqrt(L) / s2, "e2m1")
    return {
        "xT": (n((K, T)) * s).astype(np.float32),
        "wgt": np.repeat(np.random.uniform(0.5, 2.0, (8, J)), 16, axis=0).astype(np.float32),
        "zT": (n((L, T)) * s2).astype(np.float32),
        "wgt2": np.repeat(np.random.uniform(0.5, 2.0, (8, J)), 16, axis=0).astype(np.float32),
        "wa_words": p_wa[0],
        "wa_scales": p_wa[1],
        "wb_words": p_wb[0],
        "wb_scales": p_wb[1],
        "offs": striped8(np.stack([np.random.permutation(T)[:J] for _ in range(8)])),
        "offs2": striped8(np.stack([np.random.permutation(T)[:J] for _ in range(8)])),
    }


def reference(xT, wgt, zT, wgt2, wa_words, wa_scales, wb_words, wb_scales, offs, offs2):
    idx = unstriped8(offs)
    idx2 = unstriped8(offs2)
    rows = np.arange(K)
    xg = f64(wgt)[rows // 4 % 128] * f64(xT)[rows[:, None], idx[rows % 512 // 64]]
    xT_ = mxq(xg, 0, "e4m3")
    rows = np.arange(L)
    xg = f64(wgt2)[rows // 4 % 128] * f64(zT)[rows[:, None], idx2[rows % 512 // 64]]
    zT_ = mxq(xg, 0, "e4m3")
    wa_ = unpack_weight(wa_words, wa_scales, "e4m3")
    wb_ = unpack_weight(wb_words, wb_scales, "e2m1")
    ya = wa_.T @ xT_
    yb = wb_.T @ zT_
    out_0 = ya * yb
    return (out_0,) + planes(out_0)

@@ -1,0 +1,189 @@
+from contextlib import ExitStack
+
+import concourse.mybir as mybir
+
+K, N, T, J = 512, 512, 2048, 1024
+FLOPS = 2 * 2 * K * N * J
+
+F32 = mybir.dt.float32
+BF16 = mybir.dt.bfloat16
+I32 = mybir.dt.int32
+U32 = mybir.dt.uint32
+U16 = mybir.dt.uint16
+U8 = mybir.dt.uint8
+FP8X4 = mybir.dt.float8_e4m3fn_x4
+FP4X4 = mybir.dt.float4_e2m1fn_x4
+MULT = mybir.AluOpType.mult
+
+P = 128
+PACK = 4
+LANES = 16
+HALF = 512
+CHUNKS = (256, 256, 256, 128, 128)
+BANK = 512
+
+
+def interleave(nc, dst, src):
+    nc.scalar.copy(
+        out=dst.rearrange("p (c i) t -> p c t i", i=4),
+        in_=src.rearrange("p t (c i) -> p c t i", i=4),
+    )
+
+
+def tile_list_mul_noneP_kernel(
+    tc, xT, wgt, zT, wgt2, wa_words, wa_scales, wb_words, wb_scales, offs, offs2, out_0, out_1, out_2
+):
+    nc = tc.nc
+    with ExitStack() as ctx:
+        keep = ctx.enter_context(tc.tile_pool(name="keep", bufs=1))
+        psum = ctx.enter_context(tc.psum_pool(name="psum", bufs=8))
+
+        x_list = keep.tile([P, J // LANES], U16, name="x_list")
+        z_list = keep.tile([P, J // LANES], U16, name="z_list")
+        x_wgt = keep.tile([P, J], F32, name="x_wgt")
+        z_wgt = keep.tile([P, J], F32, name="z_wgt")
+        x_planes = [keep.tile([P, T], F32, name="x_plane%d" % i) for i in range(PACK)]
+        z_planes = [keep.tile([P, T], F32, name="z_plane%d" % i) for i in range(PACK)]
+        wa_raw = keep.tile([P, N], U32, name="wa_raw")
+        wb_raw = keep.tile([P, 2 * N], U8, name="wb_raw")
+        sa_raw = keep.tile([P, N], U8, name="sa_raw")
+        sb_raw = keep.tile([P, N], U8, name="sb_raw")
+        wa = keep.tile([P, N], U32, name="wa", align_bytes=64)
+        wb = keep.tile([P, 2 * N], U8, name="wb", align_bytes=64)
+        sa = keep.tile([P, N], U8, name="sa", align_bytes=64)
+        sb = keep.tile([P, N], U8, name="sb", align_bytes=64)
+
+        x_rows = xT.rearrange("(p i) t -> p i t", i=PACK)
+        z_rows = zT.rearrange("(p i) t -> p i t", i=PACK)
+
+        def load_scale_rows(raw, scales):
+            for q in range(4):
+                nc.sync.dma_start(raw[32 * q : 32 * q + 4, :].bitcast(I32), scales[0, 4 * q : 4 * q + 4, :].bitcast(I32))
+
+        nc.vector.memset(sa_raw[:].bitcast(I32), 0)
+        nc.vector.memset(sb_raw[:].bitcast(I32), 0)
+        nc.sync.dma_start(x_list[:], offs)
+        nc.sync.dma_start(x_wgt[:, :HALF], wgt[:, :HALF])
+        nc.sync.dma_start(x_planes[0][:], x_rows[:, 0, :])
+        nc.sync.dma_start(x_wgt[:, HALF:], wgt[:, HALF:])
+        load_scale_rows(sa_raw, wa_scales)
+        for i in range(1, PACK):
+            nc.sync.dma_start(x_planes[i][:], x_rows[:, i, :])
+        nc.sync.dma_start(z_list[:], offs2)
+        nc.sync.dma_start(z_wgt[:, :HALF], wgt2[:, :HALF])
+        nc.sync.dma_start(z_planes[0][:], z_rows[:, 0, :])
+        nc.sync.dma_start(z_wgt[:, HALF:], wgt2[:, HALF:])
+        nc.sync.dma_start(wa_raw[:].bitcast(I32), wa_words[0].rearrange("p n t -> p (n t)").bitcast(I32))
+        nc.sync.dma_start(z_planes[1][:], z_rows[:, 1, :])
+        load_scale_rows(sb_raw, wb_scales)
+        nc.sync.dma_start(wb_raw[:].bitcast(I32), wb_words[0].bitcast(I32))
+        for i in range(2, PACK):
+            nc.sync.dma_start(z_planes[i][:], z_rows[:, i, :])
+
+        x_g = keep.tile([P, PACK, J], F32, name="x_g")
+        x_codes = keep.tile([P, J], U32, name="x_codes", align_bytes=64)
+        z_codes = keep.tile([P, J], U32, name="z_codes", align_bytes=64)
+        x_scales = keep.tile([P, J], U8, name="x_scales", align_bytes=64)
+        z_scales = keep.tile([P, J], U8, name="z_scales", align_bytes=64)
+        z_bf = keep.tile([P, J, PACK], BF16, name="z_bf", align_bytes=64)
+        ya = keep.tile([P, PACK, J], F32, name="ya")
+        y_bf = keep.tile([P, J, PACK], BF16, name="y_bf", align_bytes=64)
+        y_codes = keep.tile([P, J], U32, name="y_codes", align_bytes=64)
+        y_scales = keep.tile([P, J], U8, name="y_scales", align_bytes=64)
+
+        def gather(dst, plane, offsets, weight, j0, j1):
+            nc.vector.tensor_tensor(
+                dst, plane[:].indirect(offsets[:, j0 // LANES : j1 // LANES]), weight[:, j0:j1], MULT
+            )
+
+        def deal_scales(dealt, raw):
+            nc.vector.tensor_copy(
+                out=dealt[:].rearrange("p (t m) -> p t m", t=PACK), in_=raw[:].rearrange("p (m t) -> p t m", t=PACK)
+            )
+
+        def quantize(codes, scales, src, j0, j1):
+            nc.vector.quantize_mx(
+                out=codes[:, j0:j1].bitcast(FP8X4), scales=scales[:, j0:j1], in_=src.rearrange("p j t -> p (j t)")
+            )
+
+        for j0 in range(0, J, HALF):
+            gather(x_g[:, 0, j0 : j0 + HALF], x_planes[0], x_list, x_wgt, j0, j0 + HALF)
+        deal_scales(sa, sa_raw)
+        for i in range(1, PACK - 1):
+            gather(x_g[:, i, :], x_planes[i], x_list, x_wgt, 0, J)
+        for j0 in range(0, J, HALF):
+            gather(x_g[:, PACK - 1, j0 : j0 + HALF], x_planes[PACK - 1], x_list, x_wgt, j0, j0 + HALF)
+
+        x_bf = [keep.tile([P, HALF, PACK], BF16, name="x_bf%d" % h, tag="stage%d" % h, align_bytes=64) for h in range(2)]
+        for h in range(2):
+            interleave(nc, x_bf[h][:], x_g[:, :, h * HALF : (h + 1) * HALF])
+            quantize(x_codes, x_scales, x_bf[h][:], h * HALF, (h + 1) * HALF)
+        nc.scalar.copy(out=wa[:].rearrange("p (t m) -> p m t", t=PACK), in_=wa_raw[:].rearrange("p (m t) -> p m t", t=PACK))
+        for j0 in range(0, J, HALF):
+            for t in range(PACK):
+                acc = psum.tile([P, BANK], F32, name="acc")
+                nc.tensor.matmul_mx(
+                    out=acc[:],
+                    lhsT=wa[:, t * P : (t + 1) * P].bitcast(FP8X4),
+                    lhsT_scale=sa[:, t * P : (t + 1) * P],
+                    rhs=x_codes[:, j0 : j0 + HALF].bitcast(FP8X4),
+                    rhs_scale=x_scales[:, j0 : j0 + HALF],
+                    start=True,
+                    stop=True,
+                )
+                nc.scalar.copy(out=ya[:, t, j0 : j0 + HALF], in_=acc[:])
+        nc.scalar.copy(
+            out=wb[:].bitcast(U16).rearrange("p (t m) -> p m t", t=PACK),
+            in_=wb_raw[:].bitcast(U16).rearrange("p (m t) -> p m t", t=PACK),
+        )
+
+        z_g = [
+            keep.tile([P, PACK, HALF], F32, name="z_g0"),
+            keep.tile([P, PACK, HALF], F32, name="z_g1", tag="stage0", align_bytes=64),
+        ]
+        for i in range(PACK - 1):
+            for h in range(2):
+                gather(z_g[h][:, i, :], z_planes[i], z_list, z_wgt, h * HALF, (h + 1) * HALF)
+            if i == 1:
+                deal_scales(sb, sb_raw)
+        starts = [sum(CHUNKS[:c]) for c in range(len(CHUNKS))]
+        for j0, width in zip(starts, CHUNKS):
+            picked = z_g[j0 // HALF][:, :, j0 % HALF : j0 % HALF + width]
+            gather(picked[:, PACK - 1, :], z_planes[PACK - 1], z_list, z_wgt, j0, j0 + width)
+            interleave(nc, z_bf[:, j0 : j0 + width, :], picked)
+
+        out_rows = out_0.rearrange("(p t) j -> p t j", t=PACK)
+        out_words = out_1[0].rearrange("p j t -> p (j t)").bitcast(I32)
+        for j0, width in zip(starts, CHUNKS):
+            j1 = j0 + width
+            y = keep.tile([P, PACK, width], F32, name="y%d" % j0)
+            quantize(z_codes, z_scales, z_bf[:, j0:j1, :], j0, j1)
+            per_bank = BANK // width
+            for t0 in range(0, PACK, per_bank):
+                acc = psum.tile([P, BANK], F32, name="acc")
+                for u in range(per_bank):
+                    t = t0 + u
+                    nc.tensor.matmul_mx(
+                        out=acc[:, u * width : (u + 1) * width],
+                        lhsT=wb[:, 2 * t * P : 2 * (t + 1) * P].bitcast(FP4X4),
+                        lhsT_scale=sb[:, t * P : (t + 1) * P],
+                        rhs=z_codes[:, j0:j1].bitcast(FP8X4),
+                        rhs_scale=z_scales[:, j0:j1],
+                        start=True,
+                        stop=True,
+                    )
+                nc.vector.tensor_tensor(
+                    y[:, t0 : t0 + per_bank, :],
+                    acc[:].rearrange("p (t j) -> p t j", t=per_bank),
+                    ya[:, t0 : t0 + per_bank, j0:j1],
+                    MULT,
+                )
+            nc.sync.dma_start(out_rows[:, :, j0:j1], y[:])
+            interleave(nc, y_bf[:, j0:j1, :], y[:])
+            quantize(y_codes, y_scales, y_bf[:, j0:j1, :], j0, j1)
+            nc.sync.dma_start(out_words[:, j0:j1], y_codes[:, j0:j1].bitcast(I32))
+        for q in range(4):
+            queue = nc.sync if q % 2 == 0 else nc.scalar
+            queue.dma_start(
+                out_2[0, 4 * q : 4 * q + 4, :].bitcast(I32), y_scales[32 * q : 32 * q + 4, :].bitcast(I32)
+            )

@@ -18,9 +18,13 @@ MULT = mybir.AluOpType.mult
 P = 128
 PACK = 4
 LANES = 16
-HALF = 512
-CHUNKS = (256, 256, 256, 128, 128)
+QUADRANTS = 4
 BANK = 512
+BANKS = 8
+HALF = J // 2
+QUARTER = J // 4
+LAST = J - J // 8
+WA_ROW = 4
 
 
 def interleave(nc, dst, src):
@@ -36,7 +40,7 @@ def tile_list_mul_noneP_kernel(
     nc = tc.nc
     with ExitStack() as ctx:
         keep = ctx.enter_context(tc.tile_pool(name="keep", bufs=1))
-        psum = ctx.enter_context(tc.psum_pool(name="psum", bufs=8))
+        psum = ctx.enter_context(tc.psum_pool(name="psum", bufs=BANKS))
 
         x_list = keep.tile([P, J // LANES], U16, name="x_list")
         z_list = keep.tile([P, J // LANES], U16, name="z_list")
@@ -46,48 +50,45 @@ def tile_list_mul_noneP_kernel(
         z_planes = [keep.tile([P, T], F32, name="z_plane%d" % i) for i in range(PACK)]
         wa_raw = keep.tile([P, N], U32, name="wa_raw")
         wb_raw = keep.tile([P, 2 * N], U8, name="wb_raw")
-        sa_raw = keep.tile([P, N], U8, name="sa_raw")
-        sb_raw = keep.tile([P, N], U8, name="sb_raw")
+        ws_raw = keep.tile([P, N], U8, name="ws_raw")
         wa = keep.tile([P, N], U32, name="wa", align_bytes=64)
         wb = keep.tile([P, 2 * N], U8, name="wb", align_bytes=64)
-        sa = keep.tile([P, N], U8, name="sa", align_bytes=64)
-        sb = keep.tile([P, N], U8, name="sb", align_bytes=64)
+        ws = keep.tile([P, N], U8, name="ws", align_bytes=64)
 
         x_rows = xT.rearrange("(p i) t -> p i t", i=PACK)
         z_rows = zT.rearrange("(p i) t -> p i t", i=PACK)
 
-        def load_scale_rows(raw, scales):
-            for q in range(4):
-                nc.sync.dma_start(raw[32 * q : 32 * q + 4, :].bitcast(I32), scales[0, 4 * q : 4 * q + 4, :].bitcast(I32))
+        def load_scale_rows(first, scales):
+            for q in range(QUADRANTS):
+                rows = ws_raw[32 * q + first : 32 * q + first + 4, :]
+                nc.sync.dma_start(rows.bitcast(I32), scales[0, 4 * q : 4 * q + 4, :].bitcast(I32))
 
-        nc.vector.memset(sa_raw[:].bitcast(I32), 0)
-        nc.vector.memset(sb_raw[:].bitcast(I32), 0)
+        nc.vector.memset(ws_raw[:].bitcast(I32), 0)
+
         nc.sync.dma_start(x_list[:], offs)
-        nc.sync.dma_start(x_wgt[:, :HALF], wgt[:, :HALF])
+        nc.sync.dma_start(x_wgt[:, :QUARTER], wgt[:, :QUARTER])
         nc.sync.dma_start(x_planes[0][:], x_rows[:, 0, :])
-        nc.sync.dma_start(x_wgt[:, HALF:], wgt[:, HALF:])
-        load_scale_rows(sa_raw, wa_scales)
-        for i in range(1, PACK):
-            nc.sync.dma_start(x_planes[i][:], x_rows[:, i, :])
-        nc.sync.dma_start(z_list[:], offs2)
-        nc.sync.dma_start(z_wgt[:, :HALF], wgt2[:, :HALF])
-        nc.sync.dma_start(z_planes[0][:], z_rows[:, 0, :])
-        nc.sync.dma_start(z_wgt[:, HALF:], wgt2[:, HALF:])
-        nc.sync.dma_start(wa_raw[:].bitcast(I32), wa_words[0].rearrange("p n t -> p (n t)").bitcast(I32))
-        nc.sync.dma_start(z_planes[1][:], z_rows[:, 1, :])
-        load_scale_rows(sb_raw, wb_scales)
+        nc.sync.dma_start(x_wgt[:, QUARTER:], wgt[:, QUARTER:])
+        load_scale_rows(WA_ROW, wa_scales)
+        nc.sync.dma_start(x_planes[1][:], x_rows[:, 1, :])
         nc.sync.dma_start(wb_raw[:].bitcast(I32), wb_words[0].bitcast(I32))
-        for i in range(2, PACK):
+        nc.sync.dma_start(x_planes[2][:], x_rows[:, 2, :])
+        load_scale_rows(0, wb_scales)
+        nc.sync.dma_start(wa_raw[:].bitcast(I32), wa_words[0].rearrange("p n t -> p (n t)").bitcast(I32))
+        nc.sync.dma_start(x_planes[3][:], x_rows[:, 3, :])
+        nc.sync.dma_start(z_list[:], offs2)
+        nc.sync.dma_start(z_wgt[:, :QUARTER], wgt2[:, :QUARTER])
+        nc.sync.dma_start(z_planes[0][:], z_rows[:, 0, :])
+        nc.sync.dma_start(z_wgt[:, QUARTER:], wgt2[:, QUARTER:])
+        for i in range(1, PACK):
             nc.sync.dma_start(z_planes[i][:], z_rows[:, i, :])
 
-        x_g = keep.tile([P, PACK, J], F32, name="x_g")
+        x_picked = keep.tile([P, PACK, J], F32, name="x_picked")
         x_codes = keep.tile([P, J], U32, name="x_codes", align_bytes=64)
         z_codes = keep.tile([P, J], U32, name="z_codes", align_bytes=64)
         x_scales = keep.tile([P, J], U8, name="x_scales", align_bytes=64)
         z_scales = keep.tile([P, J], U8, name="z_scales", align_bytes=64)
-        z_bf = keep.tile([P, J, PACK], BF16, name="z_bf", align_bytes=64)
         ya = keep.tile([P, PACK, J], F32, name="ya")
-        y_bf = keep.tile([P, J, PACK], BF16, name="y_bf", align_bytes=64)
         y_codes = keep.tile([P, J], U32, name="y_codes", align_bytes=64)
         y_scales = keep.tile([P, J], U8, name="y_scales", align_bytes=64)
 
@@ -96,93 +97,116 @@ def tile_list_mul_noneP_kernel(
                 dst, plane[:].indirect(offsets[:, j0 // LANES : j1 // LANES]), weight[:, j0:j1], MULT
             )
 
-        def deal_scales(dealt, raw):
-            nc.vector.tensor_copy(
-                out=dealt[:].rearrange("p (t m) -> p t m", t=PACK), in_=raw[:].rearrange("p (m t) -> p t m", t=PACK)
-            )
-
         def quantize(codes, scales, src, j0, j1):
             nc.vector.quantize_mx(
                 out=codes[:, j0:j1].bitcast(FP8X4), scales=scales[:, j0:j1], in_=src.rearrange("p j t -> p (j t)")
             )
 
-        for j0 in range(0, J, HALF):
-            gather(x_g[:, 0, j0 : j0 + HALF], x_planes[0], x_list, x_wgt, j0, j0 + HALF)
-        deal_scales(sa, sa_raw)
-        for i in range(1, PACK - 1):
-            gather(x_g[:, i, :], x_planes[i], x_list, x_wgt, 0, J)
-        for j0 in range(0, J, HALF):
-            gather(x_g[:, PACK - 1, j0 : j0 + HALF], x_planes[PACK - 1], x_list, x_wgt, j0, j0 + HALF)
+        for j0, j1 in ((0, QUARTER), (QUARTER, J)):
+            gather(x_picked[:, 0, j0:j1], x_planes[0], x_list, x_wgt, j0, j1)
+        nc.scalar.copy(
+            out=wb[:].bitcast(U16).rearrange("p (t m) -> p m t", t=PACK),
+            in_=wb_raw[:].bitcast(U16).rearrange("p (m t) -> p m t", t=PACK),
+        )
+        gather(x_picked[:, 1, :], x_planes[1], x_list, x_wgt, 0, J)
+        nc.scalar.copy(
+            out=wa[:].rearrange("p (t m) -> p m t", t=PACK), in_=wa_raw[:].rearrange("p (m t) -> p m t", t=PACK)
+        )
+        gather(x_picked[:, 2, :], x_planes[2], x_list, x_wgt, 0, J)
+        nc.vector.tensor_copy(
+            out=ws[:].rearrange("p (t m) -> p t m", t=PACK), in_=ws_raw[:].rearrange("p (m t) -> p t m", t=PACK)
+        )
 
-        x_bf = [keep.tile([P, HALF, PACK], BF16, name="x_bf%d" % h, tag="stage%d" % h, align_bytes=64) for h in range(2)]
-        for h in range(2):
-            interleave(nc, x_bf[h][:], x_g[:, :, h * HALF : (h + 1) * HALF])
-            quantize(x_codes, x_scales, x_bf[h][:], h * HALF, (h + 1) * HALF)
-        nc.scalar.copy(out=wa[:].rearrange("p (t m) -> p m t", t=PACK), in_=wa_raw[:].rearrange("p (m t) -> p m t", t=PACK))
-        for j0 in range(0, J, HALF):
+        x_rounded = keep.tile([P, J, PACK], BF16, name="x_rounded", align_bytes=64)
+        for j0 in range(0, J, QUARTER):
+            gather(x_picked[:, PACK - 1, j0 : j0 + QUARTER], x_planes[PACK - 1], x_list, x_wgt, j0, j0 + QUARTER)
+            interleave(nc, x_rounded[:, j0 : j0 + QUARTER, :], x_picked[:, :, j0 : j0 + QUARTER])
+        z_picked = keep.tile([P, PACK, J], F32, name="z_picked")
+
+        def gather_z(i, j0, j1):
+            gather(z_picked[:, i, j0:j1], z_planes[i], z_list, z_wgt, j0, j1)
+
+        z_first = ((0, QUARTER), (QUARTER, J))
+        for h, j0 in enumerate(range(0, J, HALF)):
+            gather_z(0, *z_first[h])
+            quantize(x_codes, x_scales, x_rounded[:, j0 : j0 + HALF, :], j0, j0 + HALF)
             for t in range(PACK):
                 acc = psum.tile([P, BANK], F32, name="acc")
                 nc.tensor.matmul_mx(
                     out=acc[:],
                     lhsT=wa[:, t * P : (t + 1) * P].bitcast(FP8X4),
-                    lhsT_scale=sa[:, t * P : (t + 1) * P],
+                    lhsT_scale=ws[WA_ROW:, t * P : (t + 1) * P],
                     rhs=x_codes[:, j0 : j0 + HALF].bitcast(FP8X4),
                     rhs_scale=x_scales[:, j0 : j0 + HALF],
                     start=True,
                     stop=True,
                 )
                 nc.scalar.copy(out=ya[:, t, j0 : j0 + HALF], in_=acc[:])
-        nc.scalar.copy(
-            out=wb[:].bitcast(U16).rearrange("p (t m) -> p m t", t=PACK),
-            in_=wb_raw[:].bitcast(U16).rearrange("p (m t) -> p m t", t=PACK),
-        )
 
-        z_g = [
-            keep.tile([P, PACK, HALF], F32, name="z_g0"),
-            keep.tile([P, PACK, HALF], F32, name="z_g1", tag="stage0", align_bytes=64),
-        ]
-        for i in range(PACK - 1):
-            for h in range(2):
-                gather(z_g[h][:, i, :], z_planes[i], z_list, z_wgt, h * HALF, (h + 1) * HALF)
-            if i == 1:
-                deal_scales(sb, sb_raw)
-        starts = [sum(CHUNKS[:c]) for c in range(len(CHUNKS))]
-        for j0, width in zip(starts, CHUNKS):
-            picked = z_g[j0 // HALF][:, :, j0 % HALF : j0 % HALF + width]
-            gather(picked[:, PACK - 1, :], z_planes[PACK - 1], z_list, z_wgt, j0, j0 + width)
-            interleave(nc, z_bf[:, j0 : j0 + width, :], picked)
+        gather_z(1, 0, J)
+        gather_z(2, 0, J)
 
         out_rows = out_0.rearrange("(p t) j -> p t j", t=PACK)
         out_words = out_1[0].rearrange("p j t -> p (j t)").bitcast(I32)
-        for j0, width in zip(starts, CHUNKS):
-            j1 = j0 + width
-            y = keep.tile([P, PACK, width], F32, name="y%d" % j0)
-            quantize(z_codes, z_scales, z_bf[:, j0:j1, :], j0, j1)
-            per_bank = BANK // width
-            for t0 in range(0, PACK, per_bank):
-                acc = psum.tile([P, BANK], F32, name="acc")
-                for u in range(per_bank):
+        y_rounded = keep.tile([P, J, PACK], BF16, name="y_rounded", align_bytes=64)
+        yb_banks = {}
+        z_rounded = {}
+
+        def pick(j0, j1):
+            gather_z(PACK - 1, j0, j1)
+            z_rounded[j0] = keep.tile(
+                [P, j1 - j0, PACK], BF16, name="z_rounded%d" % j0, tag="piece%d" % j0, align_bytes=64
+            )
+            interleave(nc, z_rounded[j0][:], z_picked[:, :, j0:j1])
+
+        def project(j0, j1):
+            width = j1 - j0
+            for t0 in range(0, PACK, BANK // width):
+                acc = psum.tile([P, BANK // width, width], F32, name="acc")
+                yb_banks[(j0, t0)] = acc
+                for u in range(BANK // width):
                     t = t0 + u
                     nc.tensor.matmul_mx(
-                        out=acc[:, u * width : (u + 1) * width],
+                        out=acc[:, u, :],
                         lhsT=wb[:, 2 * t * P : 2 * (t + 1) * P].bitcast(FP4X4),
-                        lhsT_scale=sb[:, t * P : (t + 1) * P],
+                        lhsT_scale=ws[:, t * P : (t + 1) * P],
                         rhs=z_codes[:, j0:j1].bitcast(FP8X4),
                         rhs_scale=z_scales[:, j0:j1],
                         start=True,
                         stop=True,
                     )
-                nc.vector.tensor_tensor(
-                    y[:, t0 : t0 + per_bank, :],
-                    acc[:].rearrange("p (t j) -> p t j", t=per_bank),
-                    ya[:, t0 : t0 + per_bank, j0:j1],
-                    MULT,
-                )
-            nc.sync.dma_start(out_rows[:, :, j0:j1], y[:])
-            interleave(nc, y_bf[:, j0:j1, :], y[:])
-            quantize(y_codes, y_scales, y_bf[:, j0:j1, :], j0, j1)
+
+        def quantize_z(j0, j1):
+            quantize(z_codes, z_scales, z_rounded[j0][:], j0, j1)
+
+        def multiply(j0, j1):
+            slices = BANK // (j1 - j0)
+            y = keep.tile([P, PACK, j1 - j0], F32, name="y%d" % j0, tag="piece%d" % (j0 + QUARTER), align_bytes=64)
+            for t0 in range(0, PACK, slices):
+                ts = slice(t0, t0 + slices)
+                nc.vector.tensor_tensor(y[:, ts, :], yb_banks[(j0, t0)][:], ya[:, ts, j0:j1], MULT)
+                nc.sync.dma_start(out_rows[:, ts, j0:j1], y[:, ts, :])
+            interleave(nc, y_rounded[:, j0:j1, :], y[:])
+
+        def hand_on(j0, j1):
+            quantize(y_codes, y_scales, y_rounded[:, j0:j1, :], j0, j1)
             nc.sync.dma_start(out_words[:, j0:j1], y_codes[:, j0:j1].bitcast(I32))
-        for q in range(4):
+
+        pieces = ((0, QUARTER), (QUARTER, HALF), (HALF, J - QUARTER), (J - QUARTER, LAST), (LAST, J))
+        for h0 in range(0, J, HALF):
+            quarters = range(h0, h0 + HALF, QUARTER)
+            for q0 in quarters:
+                pick(q0, q0 + QUARTER)
+            for q0 in quarters:
+                quantize_z(q0, q0 + QUARTER)
+                for j0, j1 in pieces:
+                    if q0 <= j0 < q0 + QUARTER:
+                        project(j0, j1)
+        for j0, j1 in pieces:
+            multiply(j0, j1)
+        for j0, j1 in ((0, HALF), (HALF, LAST), (LAST, J)):
+            hand_on(j0, j1)
+        for q in range(QUADRANTS):
             queue = nc.sync if q % 2 == 0 else nc.scalar
             queue.dma_start(
                 out_2[0, 4 * q : 4 * q + 4, :].bitcast(I32), y_scales[32 * q : 32 * q + 4, :].bitcast(I32)

from contextlib import ExitStack

import concourse.mybir as mybir

K, N, T, J = 512, 512, 2048, 1024
FLOPS = 2 * 2 * K * N * J

F32 = mybir.dt.float32
BF16 = mybir.dt.bfloat16
I32 = mybir.dt.int32
U32 = mybir.dt.uint32
U16 = mybir.dt.uint16
U8 = mybir.dt.uint8
FP8X4 = mybir.dt.float8_e4m3fn_x4
FP4X4 = mybir.dt.float4_e2m1fn_x4
MULT = mybir.AluOpType.mult

P = 128
PACK = 4
LANES = 16
QUADRANTS = 4
BANK = 512
BANKS = 8
HALF = J // 2
QUARTER = J // 4
LAST = J - J // 8
WA_ROW = 4


def interleave(nc, dst, src):
    nc.scalar.copy(
        out=dst.rearrange("p (c i) t -> p c t i", i=4),
        in_=src.rearrange("p t (c i) -> p c t i", i=4),
    )


def tile_list_mul_noneP_kernel(
    tc, xT, wgt, zT, wgt2, wa_words, wa_scales, wb_words, wb_scales, offs, offs2, out_0, out_1, out_2
):
    nc = tc.nc
    with ExitStack() as ctx:
        keep = ctx.enter_context(tc.tile_pool(name="keep", bufs=1))
        psum = ctx.enter_context(tc.psum_pool(name="psum", bufs=BANKS))

        x_list = keep.tile([P, J // LANES], U16, name="x_list")
        z_list = keep.tile([P, J // LANES], U16, name="z_list")
        x_wgt = keep.tile([P, J], F32, name="x_wgt")
        z_wgt = keep.tile([P, J], F32, name="z_wgt")
        x_planes = [keep.tile([P, T], F32, name="x_plane%d" % i) for i in range(PACK)]
        z_planes = [keep.tile([P, T], F32, name="z_plane%d" % i) for i in range(PACK)]
        wa_raw = keep.tile([P, N], U32, name="wa_raw")
        wb_raw = keep.tile([P, 2 * N], U8, name="wb_raw")
        ws_raw = keep.tile([P, N], U8, name="ws_raw")
        wa = keep.tile([P, N], U32, name="wa", align_bytes=64)
        wb = keep.tile([P, 2 * N], U8, name="wb", align_bytes=64)
        ws = keep.tile([P, N], U8, name="ws", align_bytes=64)

        x_rows = xT.rearrange("(p i) t -> p i t", i=PACK)
        z_rows = zT.rearrange("(p i) t -> p i t", i=PACK)

        def load_scale_rows(first, scales):
            for q in range(QUADRANTS):
                rows = ws_raw[32 * q + first : 32 * q + first + 4, :]
                nc.sync.dma_start(rows.bitcast(I32), scales[0, 4 * q : 4 * q + 4, :].bitcast(I32))

        nc.vector.memset(ws_raw[:].bitcast(I32), 0)

        nc.sync.dma_start(x_list[:], offs)
        nc.sync.dma_start(x_wgt[:, :QUARTER], wgt[:, :QUARTER])
        nc.sync.dma_start(x_planes[0][:], x_rows[:, 0, :])
        nc.sync.dma_start(x_wgt[:, QUARTER:], wgt[:, QUARTER:])
        load_scale_rows(WA_ROW, wa_scales)
        nc.sync.dma_start(x_planes[1][:], x_rows[:, 1, :])
        nc.sync.dma_start(wb_raw[:].bitcast(I32), wb_words[0].bitcast(I32))
        nc.sync.dma_start(x_planes[2][:], x_rows[:, 2, :])
        load_scale_rows(0, wb_scales)
        nc.sync.dma_start(wa_raw[:].bitcast(I32), wa_words[0].rearrange("p n t -> p (n t)").bitcast(I32))
        nc.sync.dma_start(x_planes[3][:], x_rows[:, 3, :])
        nc.sync.dma_start(z_list[:], offs2)
        nc.sync.dma_start(z_wgt[:, :QUARTER], wgt2[:, :QUARTER])
        nc.sync.dma_start(z_planes[0][:], z_rows[:, 0, :])
        nc.sync.dma_start(z_wgt[:, QUARTER:], wgt2[:, QUARTER:])
        for i in range(1, PACK):
            nc.sync.dma_start(z_planes[i][:], z_rows[:, i, :])

        x_picked = keep.tile([P, PACK, J], F32, name="x_picked")
        x_codes = keep.tile([P, J], U32, name="x_codes", align_bytes=64)
        z_codes = keep.tile([P, J], U32, name="z_codes", align_bytes=64)
        x_scales = keep.tile([P, J], U8, name="x_scales", align_bytes=64)
        z_scales = keep.tile([P, J], U8, name="z_scales", align_bytes=64)
        ya = keep.tile([P, PACK, J], F32, name="ya")
        y_codes = keep.tile([P, J], U32, name="y_codes", align_bytes=64)
        y_scales = keep.tile([P, J], U8, name="y_scales", align_bytes=64)

        def gather(dst, plane, offsets, weight, j0, j1):
            nc.vector.tensor_tensor(
                dst, plane[:].indirect(offsets[:, j0 // LANES : j1 // LANES]), weight[:, j0:j1], MULT
            )

        def quantize(codes, scales, src, j0, j1):
            nc.vector.quantize_mx(
                out=codes[:, j0:j1].bitcast(FP8X4), scales=scales[:, j0:j1], in_=src.rearrange("p j t -> p (j t)")
            )

        for j0, j1 in ((0, QUARTER), (QUARTER, J)):
            gather(x_picked[:, 0, j0:j1], x_planes[0], x_list, x_wgt, j0, j1)
        nc.scalar.copy(
            out=wb[:].bitcast(U16).rearrange("p (t m) -> p m t", t=PACK),
            in_=wb_raw[:].bitcast(U16).rearrange("p (m t) -> p m t", t=PACK),
        )
        gather(x_picked[:, 1, :], x_planes[1], x_list, x_wgt, 0, J)
        nc.scalar.copy(
            out=wa[:].rearrange("p (t m) -> p m t", t=PACK), in_=wa_raw[:].rearrange("p (m t) -> p m t", t=PACK)
        )
        gather(x_picked[:, 2, :], x_planes[2], x_list, x_wgt, 0, J)
        nc.vector.tensor_copy(
            out=ws[:].rearrange("p (t m) -> p t m", t=PACK), in_=ws_raw[:].rearrange("p (m t) -> p t m", t=PACK)
        )

        x_rounded = keep.tile([P, J, PACK], BF16, name="x_rounded", align_bytes=64)
        for j0 in range(0, J, QUARTER):
            gather(x_picked[:, PACK - 1, j0 : j0 + QUARTER], x_planes[PACK - 1], x_list, x_wgt, j0, j0 + QUARTER)
            interleave(nc, x_rounded[:, j0 : j0 + QUARTER, :], x_picked[:, :, j0 : j0 + QUARTER])
        z_picked = keep.tile([P, PACK, J], F32, name="z_picked")

        def gather_z(i, j0, j1):
            gather(z_picked[:, i, j0:j1], z_planes[i], z_list, z_wgt, j0, j1)

        z_first = ((0, QUARTER), (QUARTER, J))
        for h, j0 in enumerate(range(0, J, HALF)):
            gather_z(0, *z_first[h])
            quantize(x_codes, x_scales, x_rounded[:, j0 : j0 + HALF, :], j0, j0 + HALF)
            for t in range(PACK):
                acc = psum.tile([P, BANK], F32, name="acc")
                nc.tensor.matmul_mx(
                    out=acc[:],
                    lhsT=wa[:, t * P : (t + 1) * P].bitcast(FP8X4),
                    lhsT_scale=ws[WA_ROW:, t * P : (t + 1) * P],
                    rhs=x_codes[:, j0 : j0 + HALF].bitcast(FP8X4),
                    rhs_scale=x_scales[:, j0 : j0 + HALF],
                    start=True,
                    stop=True,
                )
                nc.scalar.copy(out=ya[:, t, j0 : j0 + HALF], in_=acc[:])

        gather_z(1, 0, J)
        gather_z(2, 0, J)

        out_rows = out_0.rearrange("(p t) j -> p t j", t=PACK)
        out_words = out_1[0].rearrange("p j t -> p (j t)").bitcast(I32)
        y_rounded = keep.tile([P, J, PACK], BF16, name="y_rounded", align_bytes=64)
        yb_banks = {}
        z_rounded = {}

        def pick(j0, j1):
            gather_z(PACK - 1, j0, j1)
            z_rounded[j0] = keep.tile(
                [P, j1 - j0, PACK], BF16, name="z_rounded%d" % j0, tag="piece%d" % j0, align_bytes=64
            )
            interleave(nc, z_rounded[j0][:], z_picked[:, :, j0:j1])

        def project(j0, j1):
            width = j1 - j0
            for t0 in range(0, PACK, BANK // width):
                acc = psum.tile([P, BANK // width, width], F32, name="acc")
                yb_banks[(j0, t0)] = acc
                for u in range(BANK // width):
                    t = t0 + u
                    nc.tensor.matmul_mx(
                        out=acc[:, u, :],
                        lhsT=wb[:, 2 * t * P : 2 * (t + 1) * P].bitcast(FP4X4),
                        lhsT_scale=ws[:, t * P : (t + 1) * P],
                        rhs=z_codes[:, j0:j1].bitcast(FP8X4),
                        rhs_scale=z_scales[:, j0:j1],
                        start=True,
                        stop=True,
                    )

        def quantize_z(j0, j1):
            quantize(z_codes, z_scales, z_rounded[j0][:], j0, j1)

        def multiply(j0, j1):
            slices = BANK // (j1 - j0)
            y = keep.tile([P, PACK, j1 - j0], F32, name="y%d" % j0, tag="piece%d" % (j0 + QUARTER), align_bytes=64)
            for t0 in range(0, PACK, slices):
                ts = slice(t0, t0 + slices)
                nc.vector.tensor_tensor(y[:, ts, :], yb_banks[(j0, t0)][:], ya[:, ts, j0:j1], MULT)
                nc.sync.dma_start(out_rows[:, ts, j0:j1], y[:, ts, :])
            interleave(nc, y_rounded[:, j0:j1, :], y[:])

        def hand_on(j0, j1):
            quantize(y_codes, y_scales, y_rounded[:, j0:j1, :], j0, j1)
            nc.sync.dma_start(out_words[:, j0:j1], y_codes[:, j0:j1].bitcast(I32))

        pieces = ((0, QUARTER), (QUARTER, HALF), (HALF, J - QUARTER), (J - QUARTER, LAST), (LAST, J))
        for h0 in range(0, J, HALF):
            quarters = range(h0, h0 + HALF, QUARTER)
            for q0 in quarters:
                pick(q0, q0 + QUARTER)
            for q0 in quarters:
                quantize_z(q0, q0 + QUARTER)
                for j0, j1 in pieces:
                    if q0 <= j0 < q0 + QUARTER:
                        project(j0, j1)
        for j0, j1 in pieces:
            multiply(j0, j1)
        for j0, j1 in ((0, HALF), (HALF, LAST), (LAST, J)):
            hand_on(j0, j1)
        for q in range(QUADRANTS):
            queue = nc.sync if q % 2 == 0 else nc.scalar
            queue.dma_start(
                out_2[0, 4 * q : 4 * q + 4, :].bitcast(I32), y_scales[32 * q : 32 * q + 4, :].bitcast(I32)
            )
